import numpy as np
import ml_dtypes


def mxq(x, axis, fmt="e4m3"):
    dtype, down = {"e4m3": (ml_dtypes.float8_e4m3fn, 7), "e5m2": (ml_dtypes.float8_e5m2, 14)}[fmt]
    v = np.moveaxis(np.asarray(x, np.float32).astype(ml_dtypes.bfloat16).astype(np.float64), axis, -1)
    blocks = v.reshape(v.shape[:-1] + (-1, 32))
    amax = np.abs(blocks).max(-1, keepdims=True)
    byte = np.maximum(np.where(amax > 0, np.frexp(amax)[1] - 1 + 127, 0) - down, 1)
    scale = np.exp2(byte - 127.0)
    codes = (blocks / scale).astype(np.float32).astype(dtype).astype(np.float64)
    return np.moveaxis((codes * scale).reshape(v.shape), -1, axis)


WIDE = False


def mx_kscale(k):
    if not WIDE:
        return np.ones(k)
    levels = np.array([10, -10, 5, -5, 0])
    if k % 512:
        return np.exp2(np.random.permutation(np.resize(levels, k // 32))).repeat(32)
    a = np.empty((k // 512, 16))
    for p in range(k // 512):
        a[p, :8] = np.random.permutation(np.resize(levels, 8))
        for g in range(8):
            far = levels[np.abs(levels - a[p, g]) >= 10]
            a[p, g + 8] = far[np.random.randint(len(far))]
    return np.exp2(a.ravel()).repeat(32)


def f64(x):
    return np.asarray(x).astype(np.float64)


def striped(idx):
    return np.tile(idx.reshape(-1, 16).T, (8, 1)).astype(np.uint16)


def unstriped(offs):
    return offs[:16].T.reshape(-1).astype(np.int64)


def striped8(idx):
    return np.concatenate([x.reshape(-1, 16).T for x in idx]).astype(np.uint16)


def runs(offs, k):
    lists = np.stack([offs[16 * r : 16 * r + 16].T.reshape(-1) for r in range(8)]).astype(np.int64)
    return lists[np.arange(k) % 512 // 64]


def pack_weight(w):
    k, n = w.shape
    w = f64(np.asarray(w, np.float32).astype(ml_dtypes.bfloat16)).reshape(k // 32, 32, n)
    amax = np.abs(w).max(1)
    byte = np.clip(np.where(amax > 0, np.frexp(amax)[1] - 1 + 127 - 7, 1), 1, 254)
    scaled = (w * np.exp2(127.0 - byte)[:, None, :]).reshape(k, n).astype(np.float32)
    words = np.ascontiguousarray(scaled.reshape(k // 512, 128, 4, n).transpose(0, 1, 3, 2)).astype(ml_dtypes.float8_e4m3fn).view(np.uint8)
    return words, np.ascontiguousarray(byte.astype(np.uint8).reshape(k // 512, 16, n))


def unpack_weight(words, scales):
    g, p, n, _ = words.shape
    vals = np.ascontiguousarray(words).view(ml_dtypes.float8_e4m3fn).astype(np.float64) * np.repeat(np.exp2(scales.astype(np.float64) - 127.0), 8, axis=1)[..., None]
    return vals.transpose(0, 1, 3, 2).reshape(g * 512, n)


def silu(v):
    return v / (1.0 + np.exp(-np.maximum(v, -700.0)))

def planes(y):
    n, m = y.shape
    v = y.astype(np.float32).astype(ml_dtypes.bfloat16).astype(np.float64).reshape(n // 32, 32, m)
    top = np.abs(v).max(1)
    byte = np.clip(np.where(top > 0, np.frexp(top)[1] - 1 + 127 - 7, 1), 1, 254)
    codes = (v * np.exp2(127.0 - byte)[:, None, :]).reshape(n, m).astype(np.float32).astype(ml_dtypes.float8_e4m3fn).view(np.uint8)
    words = codes.reshape(n // 512, 128, 4, m).transpose(0, 1, 3, 2)
    return np.ascontiguousarray(words), np.ascontiguousarray(byte.astype(np.uint8).reshape(n // 512, 16, m))


K, T, S, N, H = 512, 2048, 512, 512, 512


def setup_inputs():
    n = np.random.standard_normal
    s = mx_kscale(K)[:, None]
    u = mx_kscale(H)
    packed_xT = pack_weight(n((K, T)) * s)
    packed_w2 = pack_weight(n((H, N)) / np.sqrt(H) / u[:, None])
    return {
        "x_words": packed_xT[0],
        "x_scales": packed_xT[1],
        "w1": (n((K, H)) / np.sqrt(K) / s * u).astype(np.float32),
        "mu": np.random.uniform(0.1, 0.9, (H, 1)).astype(np.float32),
        "w2_words": packed_w2[0],
        "w2_scales": packed_w2[1],
        "offs": striped(np.random.permutation(T)[:S]),
        "back": striped8(np.random.randint(0, S, (8, S))),
    }


def reference(x_words, x_scales, w1, mu, w2_words, w2_scales, offs, back):
    xq = unpack_weight(x_words, x_scales)[:, unstriped(offs)]
    y = mxq(f64(w1), 0, "e4m3").T @ xq
    z = silu(y[np.arange(H)[:, None], runs(back, H)] + f64(mu) * (y - (y[np.arange(H)[:, None], runs(back, H)])))
    out_0 = unpack_weight(w2_words, w2_scales).T @ mxq(z, 0, "e4m3")
    return (out_0,) + planes(out_0)

@@ -1,0 +1,207 @@
+from contextlib import ExitStack
+
+import concourse.mybir as mybir
+
+K, T, S, N, H = 512, 2048, 512, 512, 512
+FLOPS = 2 * K * H * S + 2 * H * N * S
+
+F32 = mybir.dt.float32
+BF16 = mybir.dt.bfloat16
+I32 = mybir.dt.int32
+U32 = mybir.dt.uint32
+U16 = mybir.dt.uint16
+U8 = mybir.dt.uint8
+FP8X4 = mybir.dt.float8_e4m3fn_x4
+MULT = mybir.AluOpType.mult
+ADD = mybir.AluOpType.add
+COPY = mybir.ActivationFunctionType.Copy
+SILU = mybir.ActivationFunctionType.Silu
+
+P = 128
+PACK = 4
+HALF = S // 2
+CHUNK = S // 4
+GROUP = 16
+
+
+def tile_picked_tshift_silu_po_kernel(
+    tc, x_words, x_scales, w1, mu, w2_words, w2_scales, offs, back, out_0, out_1, out_2
+):
+    nc = tc.nc
+    with ExitStack() as ctx:
+        keep = ctx.enter_context(tc.tile_pool(name="keep", bufs=1))
+        psum = ctx.enter_context(tc.psum_pool(name="psum", bufs=1))
+
+        def sb(name, shape, dtype):
+            return keep.tile(shape, dtype, name=name, align_bytes=64)
+
+        offs_t = sb("offs_t", [P, S // GROUP], U16)
+        back_t = sb("back_t", [P, S // GROUP], U16)
+        w1_raw = sb("w1_raw", [P, PACK, H], F32)
+        xw_all = sb("xw_all", [P, T], U32)
+        xs_all = sb("xs_all", [P, T], U8)
+        w2w_raw = sb("w2w_raw", [P, N], I32)
+        w2s_raw = sb("w2s_raw", [P, N], U8)
+        mu_t = sb("mu_t", [P, PACK], F32)
+        rest_t = sb("rest_t", [P, PACK], F32)
+
+        nc.gpsimd.memset(xs_all[:].bitcast(I32), 0)
+        nc.vector.memset(w2s_raw[:].bitcast(I32), 0)
+        w1_rows = w1.rearrange("(p j) c -> p j c", j=PACK)
+        nc.sync.dma_start(w1_raw[:, 0:2, :], w1_rows[:, 0:2, :])
+        nc.sync.dma_start(offs_t[:], offs)
+        nc.scalar.dma_start(mu_t[:], mu.rearrange("(p t) o -> p (t o)", t=PACK))
+        for q in range(4):
+            nc.sync.dma_start(xs_all[32 * q : 32 * q + 4, :].bitcast(I32), x_scales[0, 4 * q : 4 * q + 4, :].bitcast(I32))
+        nc.sync.dma_start(w1_raw[:, 2:4, :], w1_rows[:, 2:4, :])
+        nc.sync.dma_start(xw_all[:].bitcast(I32), x_words[0].rearrange("p n r -> p (n r)").bitcast(I32))
+        nc.sync.dma_start(w2w_raw[:], w2_words[0].rearrange("p n r -> p (n r)").bitcast(I32))
+        for q in range(4):
+            nc.sync.dma_start(w2s_raw[32 * q : 32 * q + 4, :].bitcast(I32), w2_scales[0, 4 * q : 4 * q + 4, :].bitcast(I32))
+        nc.sync.dma_start(back_t[:], back)
+        nc.gpsimd.tensor_scalar(rest_t[:], mu_t[:], -1.0, 1.0, MULT, ADD)
+        warm_in = sb("warm_in", [P, 1], F32)
+        warm_out = sb("warm_out", [P, 1], F32)
+        nc.vector.memset(warm_in[:], 0.0)
+        nc.scalar.activation(warm_out[:], warm_in[:], SILU)
+        xs = sb("xs", [P, S], U8)
+        nc.vector.tensor_copy(xs[:], xs_all[:].indirect(offs_t[:]))
+
+        w1_bf = [sb("w1_bf%d" % u, [P, 2 * P * PACK], BF16) for u in range(2)]
+        w1_c = [sb("w1_c%d" % u, [P, 2 * P], U32) for u in range(2)]
+        w1_s = [sb("w1_s%d" % u, [P, 2 * P], U8) for u in range(2)]
+        src = w1_raw[:].rearrange("p j (m t) -> p m j t", t=PACK)
+        nc.vector.tensor_copy(w1_bf[0][:].rearrange("p (t m j) -> p m j t", t=2, j=PACK), src[:, :, :, 0:2])
+        nc.scalar.copy(w1_bf[1][:].rearrange("p (t m j) -> p m j t", t=2, j=PACK), src[:, :, :, 2:4])
+        for u in range(2):
+            nc.vector.quantize_mx(out=w1_c[u][:].bitcast(FP8X4), scales=w1_s[u][:], in_=w1_bf[u][:])
+
+        xw = sb("xw", [P, S], U32)
+        for h in range(2):
+            nc.vector.tensor_copy(xw[:, HALF * h : HALF * h + HALF], xw_all[:].indirect(offs_t[:, 16 * h : 16 * h + 16]))
+
+        w2w = sb("w2w", [P, N], I32)
+        nc.vector.tensor_copy(
+            w2w[:].rearrange("p (t c i) -> p c t i", t=PACK, i=4), w2w_raw[:].rearrange("p (c i t) -> p c t i", t=PACK, i=4)
+        )
+
+        w2s = sb("w2s", [P, N], U8)
+        nc.vector.tensor_copy(w2s[:].rearrange("p (t m) -> p m t", t=PACK), w2s_raw[:].rearrange("p (m t) -> p m t", t=PACK))
+
+        y = {}
+        win = [sb("win%d" % t, [P, S], F32) for t in range(PACK)]
+        own = [sb("own%d" % t, [P, S], F32) for t in range(PACK)]
+        halves = [slice(0, HALF), slice(HALF, S)]
+
+        def first(t, cols, bank):
+            acc1 = psum.tile([P, cols.stop - cols.start], F32, name="y%d" % bank, tag="bank%d" % bank)
+            wcols = slice(P * (t % 2), P * (t % 2) + P)
+            nc.tensor.matmul_mx(
+                out=acc1[:],
+                lhsT=w1_c[t // 2][:, wcols].bitcast(FP8X4),
+                lhsT_scale=w1_s[t // 2][:, wcols],
+                rhs=xw[:, cols].bitcast(FP8X4),
+                rhs_scale=xs[:, cols],
+                start=True,
+                stop=True,
+            )
+            nc.scalar.activation(win[t][:, cols], acc1[:], COPY, scale=rest_t[:, t : t + 1])
+            return acc1
+
+        def own_part(t, h):
+            nc.scalar.activation(own[t][:, halves[h]], y[t, h], COPY, scale=mu_t[:, t : t + 1])
+
+        u_half = sb("u_half", [P, PACK, HALF], F32)
+        u_q = [u_half[:, :, 0:CHUNK], u_half[:, :, CHUNK:HALF]]
+        u_q = u_q + [sb("u_q%d" % q, [P, PACK, CHUNK], F32)[:] for q in (2, 3)]
+
+        for h in range(2):
+            for t in range(2):
+                y[t, h] = first(t, halves[h], 2 * h + t)[:]
+        for t in range(2):
+            nc.vector.tensor_scalar(own[t][:, halves[0]], y[t, 0], mu_t[:, t : t + 1], None, MULT)
+        for t in (2, 3):
+            whole = first(t, slice(0, S), 2 + t)
+            y[t, 0], y[t, 1] = whole[:, halves[0]], whole[:, halves[1]]
+            own_part(t, 0)
+        for t in range(PACK):
+            nc.vector.tensor_tensor(u_half[:, t, :], win[t][:].indirect(back_t[:, 0:16]), own[t][:, halves[0]], ADD)
+        for t in range(PACK):
+            own_part(t, 1)
+
+        def shift(q, ts):
+            for t in ts:
+                nc.vector.tensor_tensor(
+                    u_q[q][:, t, :], win[t][:].indirect(back_t[:, 8 * q : 8 * q + 8]), own[t][:, CHUNK * q : CHUNK * q + CHUNK], ADD
+                )
+
+        z_bf, z_c, z_s, acc, o_f, o_bf = {}, {}, {}, {}, {}, {}
+        o_c = sb("o_c", [P, S], U32)
+        o_s = sb("o_s", [P, S], U8)
+        out_rows = out_0.rearrange("(p t) n -> p t n", t=PACK)
+        out_words = out_1[0].rearrange("p n r -> p (n r)").bitcast(I32)
+
+        def act(q):
+            z_bf[q] = sb("z_bf%d" % q, [P, PACK * CHUNK], BF16)
+            nc.scalar.activation(
+                z_bf[q][:].rearrange("p (c i t) -> p c t i", i=4, t=PACK), u_q[q].rearrange("p t (c i) -> p c t i", i=4), SILU
+            )
+
+        def second(q):
+            z_c[q] = sb("z_c%d" % q, [P, CHUNK], U32)
+            z_s[q] = sb("z_s%d" % q, [P, CHUNK], U8)
+            nc.vector.quantize_mx(out=z_c[q][:].bitcast(FP8X4), scales=z_s[q][:], in_=z_bf[q][:])
+            acc[q] = psum.tile([P, PACK, CHUNK], F32, name="acc%d" % q, tag="bank%d" % ((6 + q) % 8))
+            for t in range(PACK):
+                nc.tensor.matmul_mx(
+                    out=acc[q][:, t, :],
+                    lhsT=w2w[:, P * t : P * t + P].bitcast(FP8X4),
+                    lhsT_scale=w2s[:, P * t : P * t + P],
+                    rhs=z_c[q][:].bitcast(FP8X4),
+                    rhs_scale=z_s[q][:],
+                    start=True,
+                    stop=True,
+                )
+
+        def leave(q):
+            o_f[q] = sb("o_f%d" % q, [P, PACK, CHUNK], F32)
+            nc.scalar.copy(o_f[q][:], acc[q][:])
+            nc.sync.dma_start(out_rows[:, :, CHUNK * q : CHUNK * q + CHUNK], o_f[q][:])
+
+        def weave(q):
+            o_bf[q] = sb("o_bf%d" % q, [P, PACK * CHUNK], BF16)
+            nc.vector.tensor_copy(
+                o_bf[q][:].rearrange("p (c i t) -> p c t i", i=4, t=PACK), o_f[q][:].rearrange("p t (c i) -> p c t i", i=4)
+            )
+
+        def planes(q):
+            cols = slice(CHUNK * q, CHUNK * q + CHUNK)
+            nc.vector.quantize_mx(out=o_c[:, cols].bitcast(FP8X4), scales=o_s[:, cols], in_=o_bf[q][:])
+            nc.sync.dma_start(out_words[:, cols], o_c[:, cols].bitcast(I32))
+
+        shift(2, range(4))
+        act(0)
+        act(1)
+        second(0)
+        shift(3, (0, 1))
+        act(2)
+        second(1)
+        shift(3, (2, 3))
+        leave(0)
+        second(2)
+        act(3)
+        weave(0)
+        second(3)
+        planes(0)
+        leave(1)
+        leave(2)
+        leave(3)
+        weave(1)
+        weave(2)
+        planes(1)
+        planes(2)
+        weave(3)
+        planes(3)
+        for q in range(4):
+            eng = nc.sync if q % 2 == 0 else nc.scalar
+            eng.dma_start(out_2[0, 4 * q : 4 * q + 4, :].bitcast(I32), o_s[32 * q : 32 * q + 4, :].bitcast(I32))

@@ -48,8 +48,8 @@ def tile_picked_tshift_silu_po_kernel(
         nc.gpsimd.memset(xs_all[:].bitcast(I32), 0)
         nc.vector.memset(w2s_raw[:].bitcast(I32), 0)
         w1_rows = w1.rearrange("(p j) c -> p j c", j=PACK)
-        nc.sync.dma_start(w1_raw[:, 0:2, :], w1_rows[:, 0:2, :])
         nc.sync.dma_start(offs_t[:], offs)
+        nc.sync.dma_start(w1_raw[:, 0:2, :], w1_rows[:, 0:2, :])
         nc.scalar.dma_start(mu_t[:], mu.rearrange("(p t) o -> p (t o)", t=PACK))
         for q in range(4):
             nc.sync.dma_start(xs_all[32 * q : 32 * q + 4, :].bitcast(I32), x_scales[0, 4 * q : 4 * q + 4, :].bitcast(I32))
@@ -113,7 +113,14 @@ def tile_picked_tshift_silu_po_kernel(
 
         u_half = sb("u_half", [P, PACK, HALF], F32)
         u_q = [u_half[:, :, 0:CHUNK], u_half[:, :, CHUNK:HALF]]
-        u_q = u_q + [sb("u_q%d" % q, [P, PACK, CHUNK], F32)[:] for q in (2, 3)]
+        u_flat = [sb("u_q%d" % q, [P, PACK * CHUNK], F32) for q in (2, 3)]
+        u_q = u_q + [u_flat[i][:].rearrange("p (t n) -> p t n", t=PACK) for i in range(2)]
+        z_bf = [
+            u_flat[0][:, 2 * CHUNK : 4 * CHUNK].bitcast(BF16),
+            u_flat[1][:, 0 : 2 * CHUNK].bitcast(BF16),
+            sb("z_bf2", [P, PACK * CHUNK], BF16)[:],
+            sb("z_bf3", [P, PACK * CHUNK], BF16)[:],
+        ]
 
         for h in range(2):
             for t in range(2):
@@ -132,29 +139,32 @@ def tile_picked_tshift_silu_po_kernel(
         def shift(q, ts):
             for t in ts:
                 nc.vector.tensor_tensor(
-                    u_q[q][:, t, :], win[t][:].indirect(back_t[:, 8 * q : 8 * q + 8]), own[t][:, CHUNK * q : CHUNK * q + CHUNK], ADD
+                    u_flat[q - 2][:, CHUNK * t : CHUNK * t + CHUNK], win[t][:].indirect(back_t[:, 8 * q : 8 * q + 8]), own[t][:, CHUNK * q : CHUNK * q + CHUNK], ADD
                 )
 
-        z_bf, z_c, z_s, acc, o_f, o_bf = {}, {}, {}, {}, {}, {}
+        z_c, z_s, acc, o_f, o_bf = {}, {}, {}, {}, {}
         o_c = sb("o_c", [P, S], U32)
         o_s = sb("o_s", [P, S], U8)
         out_rows = out_0.rearrange("(p t) n -> p t n", t=PACK)
         out_words = out_1[0].rearrange("p n r -> p (n r)").bitcast(I32)
 
         def act(q):
-            z_bf[q] = sb("z_bf%d" % q, [P, PACK * CHUNK], BF16)
             nc.scalar.activation(
-                z_bf[q][:].rearrange("p (c i t) -> p c t i", i=4, t=PACK), u_q[q].rearrange("p t (c i) -> p c t i", i=4), SILU
+                z_bf[q].rearrange("p (c i t) -> p c t i", i=4, t=PACK), u_q[q].rearrange("p t (c i) -> p c t i", i=4), SILU
             )
 
         def second(q):
             z_c[q] = sb("z_c%d" % q, [P, CHUNK], U32)
             z_s[q] = sb("z_s%d" % q, [P, CHUNK], U8)
-            nc.vector.quantize_mx(out=z_c[q][:].bitcast(FP8X4), scales=z_s[q][:], in_=z_bf[q][:])
-            acc[q] = psum.tile([P, PACK, CHUNK], F32, name="acc%d" % q, tag="bank%d" % ((6 + q) % 8))
+            nc.vector.quantize_mx(out=z_c[q][:].bitcast(FP8X4), scales=z_s[q][:], in_=z_bf[q])
+            if q < 3:
+                whole_bank = psum.tile([P, PACK, CHUNK], F32, name="acc%d" % q, tag="bank%d" % ((6 + q) % 8))
+                acc[q] = [whole_bank[:, 0:2, :], whole_bank[:, 2:4, :], whole_bank[:]]
+            else:
+                acc[q] = [psum.tile([P, 2, CHUNK], F32, name="acc3%d" % i, tag="bank%d" % (1 + i))[:] for i in range(2)]
             for t in range(PACK):
                 nc.tensor.matmul_mx(
-                    out=acc[q][:, t, :],
+                    out=acc[q][t // 2][:, t % 2, :],
                     lhsT=w2w[:, P * t : P * t + P].bitcast(FP8X4),
                     lhsT_scale=w2s[:, P * t : P * t + P],
                     rhs=z_c[q][:].bitcast(FP8X4),
@@ -165,7 +175,11 @@ def tile_picked_tshift_silu_po_kernel(
 
         def leave(q):
             o_f[q] = sb("o_f%d" % q, [P, PACK, CHUNK], F32)
-            nc.scalar.copy(o_f[q][:], acc[q][:])
+            if q < 3:
+                nc.scalar.copy(o_f[q][:], acc[q][2])
+            else:
+                nc.vector.tensor_copy(o_f[q][:, 0:2, :], acc[q][0])
+                nc.scalar.copy(o_f[q][:, 2:4, :], acc[q][1])
             nc.sync.dma_start(out_rows[:, :, CHUNK * q : CHUNK * q + CHUNK], o_f[q][:])
 
         def weave(q):
@@ -177,31 +191,33 @@ def tile_picked_tshift_silu_po_kernel(
         def planes(q):
             cols = slice(CHUNK * q, CHUNK * q + CHUNK)
             nc.vector.quantize_mx(out=o_c[:, cols].bitcast(FP8X4), scales=o_s[:, cols], in_=o_bf[q][:])
-            nc.sync.dma_start(out_words[:, cols], o_c[:, cols].bitcast(I32))
+            if q >= 2:
+                wcols = slice(0, 3 * CHUNK) if q == 2 else cols
+                nc.sync.dma_start(out_words[:, wcols], o_c[:, wcols].bitcast(I32))
 
-        shift(2, range(4))
+        shift(2, (0, 1))
         act(0)
-        act(1)
         second(0)
-        shift(3, (0, 1))
-        act(2)
+        act(1)
+        shift(2, (2, 3))
         second(1)
-        shift(3, (2, 3))
         leave(0)
+        act(2)
+        shift(3, range(4))
         second(2)
-        act(3)
-        weave(0)
-        second(3)
-        planes(0)
         leave(1)
+        act(3)
+        second(3)
+        weave(0)
+        planes(0)
         leave(2)
-        leave(3)
         weave(1)
-        weave(2)
         planes(1)
+        leave(3)
+        weave(2)
         planes(2)
         weave(3)
         planes(3)
         for q in range(4):
-            eng = nc.sync if q % 2 == 0 else nc.scalar
+            eng = nc.scalar if q % 2 == 0 else nc.sync
             eng.dma_start(out_2[0, 4 * q : 4 * q + 4, :].bitcast(I32), o_s[32 * q : 32 * q + 4, :].bitcast(I32))

@@ -48,8 +48,8 @@ def tile_picked_tshift_silu_po_kernel(
         nc.gpsimd.memset(xs_all[:].bitcast(I32), 0)
         nc.vector.memset(w2s_raw[:].bitcast(I32), 0)
         w1_rows = w1.rearrange("(p j) c -> p j c", j=PACK)
-        nc.sync.dma_start(offs_t[:], offs)
         nc.sync.dma_start(w1_raw[:, 0:2, :], w1_rows[:, 0:2, :])
+        nc.sync.dma_start(offs_t[:], offs)
         nc.scalar.dma_start(mu_t[:], mu.rearrange("(p t) o -> p (t o)", t=PACK))
         for q in range(4):
             nc.sync.dma_start(xs_all[32 * q : 32 * q + 4, :].bitcast(I32), x_scales[0, 4 * q : 4 * q + 4, :].bitcast(I32))

@@ -50,14 +50,16 @@ def tile_picked_tshift_silu_po_kernel(
         w1_rows = w1.rearrange("(p j) c -> p j c", j=PACK)
         nc.sync.dma_start(w1_raw[:, 0:2, :], w1_rows[:, 0:2, :])
         nc.sync.dma_start(offs_t[:], offs)
-        nc.scalar.dma_start(mu_t[:], mu.rearrange("(p t) o -> p (t o)", t=PACK))
-        for q in range(4):
-            nc.sync.dma_start(xs_all[32 * q : 32 * q + 4, :].bitcast(I32), x_scales[0, 4 * q : 4 * q + 4, :].bitcast(I32))
+        xs_rows = x_scales[0].rearrange("(q r) n -> r q n", r=4)
+        for r in range(4):
+            nc.sync.dma_start(xs_all[r:P:32, :].bitcast(I32), xs_rows[r].bitcast(I32))
         nc.sync.dma_start(w1_raw[:, 2:4, :], w1_rows[:, 2:4, :])
         nc.sync.dma_start(xw_all[:].bitcast(I32), x_words[0].rearrange("p n r -> p (n r)").bitcast(I32))
+        nc.sync.dma_start(mu_t[:], mu.rearrange("(p t) o -> p (t o)", t=PACK))
         nc.sync.dma_start(w2w_raw[:], w2_words[0].rearrange("p n r -> p (n r)").bitcast(I32))
-        for q in range(4):
-            nc.sync.dma_start(w2s_raw[32 * q : 32 * q + 4, :].bitcast(I32), w2_scales[0, 4 * q : 4 * q + 4, :].bitcast(I32))
+        w2s_rows = w2_scales[0].rearrange("(q r) n -> r q n", r=4)
+        for r in range(4):
+            nc.sync.dma_start(w2s_raw[r:P:32, :].bitcast(I32), w2s_rows[r].bitcast(I32))
         nc.sync.dma_start(back_t[:], back)
         nc.gpsimd.tensor_scalar(rest_t[:], mu_t[:], -1.0, 1.0, MULT, ADD)
         warm_in = sb("warm_in", [P, 1], F32)
@@ -191,8 +193,8 @@ def tile_picked_tshift_silu_po_kernel(
         def planes(q):
             cols = slice(CHUNK * q, CHUNK * q + CHUNK)
             nc.vector.quantize_mx(out=o_c[:, cols].bitcast(FP8X4), scales=o_s[:, cols], in_=o_bf[q][:])
-            if q >= 2:
-                wcols = slice(0, 3 * CHUNK) if q == 2 else cols
+            if q >= 1:
+                wcols = slice(0, 2 * CHUNK) if q == 1 else cols
                 nc.sync.dma_start(out_words[:, wcols], o_c[:, wcols].bitcast(I32))
 
         shift(2, (0, 1))
@@ -218,6 +220,7 @@ def tile_picked_tshift_silu_po_kernel(
         planes(2)
         weave(3)
         planes(3)
-        for q in range(4):
-            eng = nc.scalar if q % 2 == 0 else nc.sync
-            eng.dma_start(out_2[0, 4 * q : 4 * q + 4, :].bitcast(I32), o_s[32 * q : 32 * q + 4, :].bitcast(I32))
+        out_scales = out_2[0].rearrange("(q r) n -> r q n", r=4)
+        for r in range(4):
+            eng = nc.scalar if r % 2 == 0 else nc.sync
+            eng.dma_start(out_scales[r].bitcast(I32), o_s[r:P:32, :].bitcast(I32))

@@ -88,7 +88,7 @@ def tile_picked_tshift_silu_po_kernel(
         )
 
         w2s = sb("w2s", [P, N], U8)
-        nc.vector.tensor_copy(w2s[:].rearrange("p (t m) -> p m t", t=PACK), w2s_raw[:].rearrange("p (m t) -> p m t", t=PACK))
+        nc.vector.tensor_copy(w2s[:].rearrange("p (t m) -> p t m", t=PACK), w2s_raw[:].rearrange("p (m t) -> p t m", t=PACK))
 
         y = {}
         win = [sb("win%d" % t, [P, S], F32) for t in range(PACK)]
@@ -113,15 +113,13 @@ def tile_picked_tshift_silu_po_kernel(
         def own_part(t, h):
             nc.scalar.activation(own[t][:, halves[h]], y[t, h], COPY, scale=mu_t[:, t : t + 1])
 
-        u_half = sb("u_half", [P, PACK, HALF], F32)
-        u_q = [u_half[:, :, 0:CHUNK], u_half[:, :, CHUNK:HALF]]
-        u_flat = [sb("u_q%d" % q, [P, PACK * CHUNK], F32) for q in (2, 3)]
-        u_q = u_q + [u_flat[i][:].rearrange("p (t n) -> p t n", t=PACK) for i in range(2)]
-        z_bf = [
-            u_flat[0][:, 2 * CHUNK : 4 * CHUNK].bitcast(BF16),
-            u_flat[1][:, 0 : 2 * CHUNK].bitcast(BF16),
-            sb("z_bf2", [P, PACK * CHUNK], BF16)[:],
-            sb("z_bf3", [P, PACK * CHUNK], BF16)[:],
+        u_ring = sb("u_ring", [P, 10 * CHUNK], F32)
+        u_half = u_ring[:, 2 * CHUNK : 10 * CHUNK].rearrange("p (t n) -> p t n", t=PACK)
+        u_q = [
+            u_half[:, :, 0:CHUNK],
+            u_half[:, :, CHUNK:HALF],
+            sb("u_q2", [P, PACK, CHUNK], F32)[:],
+            u_ring[:, 0 : PACK * CHUNK].rearrange("p (t n) -> p t n", t=PACK),
         ]
 
         for h in range(2):
@@ -141,85 +139,99 @@ def tile_picked_tshift_silu_po_kernel(
         def shift(q, ts):
             for t in ts:
                 nc.vector.tensor_tensor(
-                    u_flat[q - 2][:, CHUNK * t : CHUNK * t + CHUNK], win[t][:].indirect(back_t[:, 8 * q : 8 * q + 8]), own[t][:, CHUNK * q : CHUNK * q + CHUNK], ADD
+                    u_q[q][:, t, :], win[t][:].indirect(back_t[:, 8 * q : 8 * q + 8]), own[t][:, CHUNK * q : CHUNK * q + CHUNK], ADD
                 )
 
-        z_c, z_s, acc, o_f, o_bf = {}, {}, {}, {}, {}
+        z_bf, acc = {}, {}
+        o_f = [sb("o_f%d" % q, [P, PACK, CHUNK], F32) for q in range(4)]
+        o_bf = sb("o_bf", [P, PACK * S], BF16)
         o_c = sb("o_c", [P, S], U32)
         o_s = sb("o_s", [P, S], U8)
         out_rows = out_0.rearrange("(p t) n -> p t n", t=PACK)
         out_words = out_1[0].rearrange("p n r -> p (n r)").bitcast(I32)
 
-        def act(q):
+        def within(lo, hi):
+            return slice(lo % CHUNK, lo % CHUNK + hi - lo)
+
+        def act(lo, hi):
+            z_bf[lo] = sb("z_bf%d" % lo, [P, PACK * (hi - lo)], BF16)
             nc.scalar.activation(
-                z_bf[q].rearrange("p (c i t) -> p c t i", i=4, t=PACK), u_q[q].rearrange("p t (c i) -> p c t i", i=4), SILU
+                z_bf[lo][:].rearrange("p (c i t) -> p c t i", i=4, t=PACK),
+                u_q[lo // CHUNK][:, :, within(lo, hi)].rearrange("p t (c i) -> p c t i", i=4),
+                SILU,
             )
 
-        def second(q):
-            z_c[q] = sb("z_c%d" % q, [P, CHUNK], U32)
-            z_s[q] = sb("z_s%d" % q, [P, CHUNK], U8)
-            nc.vector.quantize_mx(out=z_c[q][:].bitcast(FP8X4), scales=z_s[q][:], in_=z_bf[q])
-            if q < 3:
-                whole_bank = psum.tile([P, PACK, CHUNK], F32, name="acc%d" % q, tag="bank%d" % ((6 + q) % 8))
-                acc[q] = [whole_bank[:, 0:2, :], whole_bank[:, 2:4, :], whole_bank[:]]
-            else:
-                acc[q] = [psum.tile([P, 2, CHUNK], F32, name="acc3%d" % i, tag="bank%d" % (1 + i))[:] for i in range(2)]
+        def second(lo, hi, banks):
+            z_c = sb("z_c%d" % lo, [P, hi - lo], U32)
+            z_s = sb("z_s%d" % lo, [P, hi - lo], U8)
+            nc.vector.quantize_mx(out=z_c[:].bitcast(FP8X4), scales=z_s[:], in_=z_bf[lo][:])
+            per = PACK // len(banks)
+            acc[lo] = [psum.tile([P, per, hi - lo], F32, name="acc%d_%d" % (lo, b), tag="bank%d" % b) for b in banks]
             for t in range(PACK):
                 nc.tensor.matmul_mx(
-                    out=acc[q][t // 2][:, t % 2, :],
+                    out=acc[lo][t // per][:, t % per, :],
                     lhsT=w2w[:, P * t : P * t + P].bitcast(FP8X4),
                     lhsT_scale=w2s[:, P * t : P * t + P],
-                    rhs=z_c[q][:].bitcast(FP8X4),
-                    rhs_scale=z_s[q][:],
+                    rhs=z_c[:].bitcast(FP8X4),
+                    rhs_scale=z_s[:],
                     start=True,
                     stop=True,
                 )
 
-        def leave(q):
-            o_f[q] = sb("o_f%d" % q, [P, PACK, CHUNK], F32)
-            if q < 3:
-                nc.scalar.copy(o_f[q][:], acc[q][2])
-            else:
-                nc.vector.tensor_copy(o_f[q][:, 0:2, :], acc[q][0])
-                nc.scalar.copy(o_f[q][:, 2:4, :], acc[q][1])
+        def leave(lo, hi, engines):
+            per = PACK // len(engines)
+            for i in range(len(engines)):
+                dst = o_f[lo // CHUNK][:, per * i : per * i + per, within(lo, hi)]
+                if engines[i] == "V":
+                    nc.vector.tensor_copy(dst, acc[lo][i][:])
+                else:
+                    nc.scalar.copy(dst, acc[lo][i][:])
+
+        def store(q):
             nc.sync.dma_start(out_rows[:, :, CHUNK * q : CHUNK * q + CHUNK], o_f[q][:])
 
-        def weave(q):
-            o_bf[q] = sb("o_bf%d" % q, [P, PACK * CHUNK], BF16)
+        def weave(lo, hi):
             nc.vector.tensor_copy(
-                o_bf[q][:].rearrange("p (c i t) -> p c t i", i=4, t=PACK), o_f[q][:].rearrange("p t (c i) -> p c t i", i=4)
+                o_bf[:, PACK * lo : PACK * hi].rearrange("p (c i t) -> p c t i", i=4, t=PACK),
+                o_f[lo // CHUNK][:, :, within(lo, hi)].rearrange("p t (c i) -> p c t i", i=4),
             )
 
-        def planes(q):
-            cols = slice(CHUNK * q, CHUNK * q + CHUNK)
-            nc.vector.quantize_mx(out=o_c[:, cols].bitcast(FP8X4), scales=o_s[:, cols], in_=o_bf[q][:])
-            if q >= 1:
-                wcols = slice(0, 2 * CHUNK) if q == 1 else cols
-                nc.sync.dma_start(out_words[:, wcols], o_c[:, wcols].bitcast(I32))
+        def planes(lo, hi):
+            nc.vector.quantize_mx(out=o_c[:, lo:hi].bitcast(FP8X4), scales=o_s[:, lo:hi], in_=o_bf[:, PACK * lo : PACK * hi])
 
-        shift(2, (0, 1))
-        act(0)
-        second(0)
-        act(1)
-        shift(2, (2, 3))
-        second(1)
-        leave(0)
-        act(2)
+        def words(lo, hi):
+            nc.sync.dma_start(out_words[:, lo:hi], o_c[:, lo:hi].bitcast(I32))
+
+        act(0, 128)
+        second(0, 128, [6])
+        act(128, 256)
+        second(128, 256, [7])
+        shift(2, range(4))
+        act(256, 384)
+        second(256, 384, [0])
         shift(3, range(4))
-        second(2)
-        leave(1)
-        act(3)
-        second(3)
-        weave(0)
-        planes(0)
-        leave(2)
-        weave(1)
-        planes(1)
-        leave(3)
-        weave(2)
-        planes(2)
-        weave(3)
-        planes(3)
+        act(384, 512)
+        second(384, 512, [1, 2])
+        leave(0, 128, "V")
+        store(0)
+        leave(128, 256, "S")
+        store(1)
+        leave(256, 384, "S")
+        store(2)
+        leave(384, 512, "VS")
+        store(3)
+        weave(0, 128)
+        weave(128, 256)
+        planes(0, 256)
+        words(0, 256)
+        weave(256, 384)
+        weave(384, 448)
+        planes(256, 384)
+        words(256, 384)
+        weave(448, 512)
+        planes(384, 448)
+        planes(448, 512)
+        words(384, 512)
         out_scales = out_2[0].rearrange("(q r) n -> r q n", r=4)
         for r in range(4):
             eng = nc.scalar if r % 2 == 0 else nc.sync

@@ -113,13 +113,13 @@ def tile_picked_tshift_silu_po_kernel(
         def own_part(t, h):
             nc.scalar.activation(own[t][:, halves[h]], y[t, h], COPY, scale=mu_t[:, t : t + 1])
 
-        u_ring = sb("u_ring", [P, 10 * CHUNK], F32)
-        u_half = u_ring[:, 2 * CHUNK : 10 * CHUNK].rearrange("p (t n) -> p t n", t=PACK)
+        u_ring = sb("u_ring", [P, 11 * CHUNK], F32)
+        u_half = u_ring[:, 3 * CHUNK : 11 * CHUNK].rearrange("p (t n) -> p t n", t=PACK)
         u_q = [
             u_half[:, :, 0:CHUNK],
             u_half[:, :, CHUNK:HALF],
-            sb("u_q2", [P, PACK, CHUNK], F32)[:],
             u_ring[:, 0 : PACK * CHUNK].rearrange("p (t n) -> p t n", t=PACK),
+            u_half[:, :, CHUNK:HALF],
         ]
 
         for h in range(2):
@@ -131,10 +131,8 @@ def tile_picked_tshift_silu_po_kernel(
             whole = first(t, slice(0, S), 2 + t)
             y[t, 0], y[t, 1] = whole[:, halves[0]], whole[:, halves[1]]
             own_part(t, 0)
-        for t in range(PACK):
+        for t in range(PACK - 1):
             nc.vector.tensor_tensor(u_half[:, t, :], win[t][:].indirect(back_t[:, 0:16]), own[t][:, halves[0]], ADD)
-        for t in range(PACK):
-            own_part(t, 1)
 
         def shift(q, ts):
             for t in ts:
@@ -202,28 +200,34 @@ def tile_picked_tshift_silu_po_kernel(
         def words(lo, hi):
             nc.sync.dma_start(out_words[:, lo:hi], o_c[:, lo:hi].bitcast(I32))
 
+        shift(0, (3,))
         act(0, 128)
         second(0, 128, [6])
+        shift(1, (3,))
+        leave(0, 128, "S")
+        store(0)
         act(128, 256)
         second(128, 256, [7])
+        for t in range(PACK):
+            own_part(t, 1)
+        leave(128, 256, "S")
+        store(1)
         shift(2, range(4))
         act(256, 384)
         second(256, 384, [0])
         shift(3, range(4))
         act(384, 512)
         second(384, 512, [1, 2])
-        leave(0, 128, "V")
-        store(0)
-        leave(128, 256, "S")
-        store(1)
         leave(256, 384, "S")
         store(2)
         leave(384, 512, "VS")
         store(3)
         weave(0, 128)
         weave(128, 256)
-        planes(0, 256)
-        words(0, 256)
+        planes(0, 128)
+        words(0, 128)
+        planes(128, 256)
+        words(128, 256)
         weave(256, 384)
         weave(384, 448)
         planes(256, 384)

@@ -225,17 +225,15 @@ def tile_picked_tshift_silu_po_kernel(
         weave(0, 128)
         weave(128, 256)
         planes(0, 128)
-        words(0, 128)
         planes(128, 256)
-        words(128, 256)
+        words(0, 256)
         weave(256, 384)
         weave(384, 448)
         planes(256, 384)
-        words(256, 384)
         weave(448, 512)
         planes(384, 448)
         planes(448, 512)
-        words(384, 512)
+        words(256, 512)
         out_scales = out_2[0].rearrange("(q r) n -> r q n", r=4)
         for r in range(4):
             eng = nc.scalar if r % 2 == 0 else nc.sync

@@ -32,8 +32,8 @@ def tile_picked_tshift_silu_po_kernel(
         keep = ctx.enter_context(tc.tile_pool(name="keep", bufs=1))
         psum = ctx.enter_context(tc.psum_pool(name="psum", bufs=1))
 
-        def sb(name, shape, dtype):
-            return keep.tile(shape, dtype, name=name, align_bytes=64)
+        def sb(name, shape, dtype, tag=None):
+            return keep.tile(shape, dtype, name=name, tag=tag or name, align_bytes=64)
 
         offs_t = sb("offs_t", [P, S // GROUP], U16)
         back_t = sb("back_t", [P, S // GROUP], U16)
@@ -82,36 +82,48 @@ def tile_picked_tshift_silu_po_kernel(
         for h in range(2):
             nc.vector.tensor_copy(xw[:, HALF * h : HALF * h + HALF], xw_all[:].indirect(offs_t[:, 16 * h : 16 * h + 16]))
 
-        w2w = sb("w2w", [P, N], I32)
-        nc.vector.tensor_copy(
-            w2w[:].rearrange("p (t c i) -> p c t i", t=PACK, i=4), w2w_raw[:].rearrange("p (c i t) -> p c t i", t=PACK, i=4)
-        )
-
-        w2s = sb("w2s", [P, N], U8)
-        nc.vector.tensor_copy(w2s[:].rearrange("p (t m) -> p t m", t=PACK), w2s_raw[:].rearrange("p (m t) -> p t m", t=PACK))
 
         y = {}
         win = [sb("win%d" % t, [P, S], F32) for t in range(PACK)]
         own = [sb("own%d" % t, [P, S], F32) for t in range(PACK)]
         halves = [slice(0, HALF), slice(HALF, S)]
+        w2w = sb("w2w", [P, N], I32)
+        dealt = {}
 
-        def first(t, cols, bank):
-            acc1 = psum.tile([P, cols.stop - cols.start], F32, name="y%d" % bank, tag="bank%d" % bank)
+        def deal_words():
+            nc.gpsimd.tensor_copy(
+                w2w[:].rearrange("p (t c i) -> p c t i", t=PACK, i=4), w2w_raw[:].rearrange("p (c i t) -> p c t i", t=PACK, i=4)
+            )
+
+        def deal_bytes():
+            dealt["w2s"] = sb("w2s", [P, N], U8)
+            nc.gpsimd.tensor_copy(
+                dealt["w2s"][:].rearrange("p (t m) -> p t m", t=PACK), w2s_raw[:].rearrange("p (m t) -> p t m", t=PACK)
+            )
+
+        def first(t, h, bank, engine="S"):
+            acc1 = psum.tile([P, HALF], F32, name="y%d" % bank, tag="bank%d" % bank)
             wcols = slice(P * (t % 2), P * (t % 2) + P)
             nc.tensor.matmul_mx(
                 out=acc1[:],
                 lhsT=w1_c[t // 2][:, wcols].bitcast(FP8X4),
                 lhsT_scale=w1_s[t // 2][:, wcols],
-                rhs=xw[:, cols].bitcast(FP8X4),
-                rhs_scale=xs[:, cols],
+                rhs=xw[:, halves[h]].bitcast(FP8X4),
+                rhs_scale=xs[:, halves[h]],
                 start=True,
                 stop=True,
             )
-            nc.scalar.activation(win[t][:, cols], acc1[:], COPY, scale=rest_t[:, t : t + 1])
-            return acc1
+            if engine == "V":
+                nc.vector.tensor_scalar(win[t][:, halves[h]], acc1[:], rest_t[:, t : t + 1], None, MULT)
+            else:
+                nc.scalar.activation(win[t][:, halves[h]], acc1[:], COPY, scale=rest_t[:, t : t + 1])
+            y[t, h] = acc1[:]
 
         def own_part(t, h):
             nc.scalar.activation(own[t][:, halves[h]], y[t, h], COPY, scale=mu_t[:, t : t + 1])
+
+        def own_vec(t, h):
+            nc.vector.tensor_scalar(own[t][:, halves[h]], y[t, h], mu_t[:, t : t + 1], None, MULT)
 
         u_ring = sb("u_ring", [P, 11 * CHUNK], F32)
         u_half = u_ring[:, 3 * CHUNK : 11 * CHUNK].rearrange("p (t n) -> p t n", t=PACK)
@@ -122,16 +134,7 @@ def tile_picked_tshift_silu_po_kernel(
             u_half[:, :, CHUNK:HALF],
         ]
 
-        for h in range(2):
-            for t in range(2):
-                y[t, h] = first(t, halves[h], 2 * h + t)[:]
-        for t in range(2):
-            nc.vector.tensor_scalar(own[t][:, halves[0]], y[t, 0], mu_t[:, t : t + 1], None, MULT)
-        for t in (2, 3):
-            whole = first(t, slice(0, S), 2 + t)
-            y[t, 0], y[t, 1] = whole[:, halves[0]], whole[:, halves[1]]
-            own_part(t, 0)
-        for t in range(PACK - 1):
+        def wide(t):
             nc.vector.tensor_tensor(u_half[:, t, :], win[t][:].indirect(back_t[:, 0:16]), own[t][:, halves[0]], ADD)
 
         def shift(q, ts):
@@ -139,6 +142,7 @@ def tile_picked_tshift_silu_po_kernel(
                 nc.vector.tensor_tensor(
                     u_q[q][:, t, :], win[t][:].indirect(back_t[:, 8 * q : 8 * q + 8]), own[t][:, CHUNK * q : CHUNK * q + CHUNK], ADD
                 )
+
 
         z_bf, acc = {}, {}
         o_f = [sb("o_f%d" % q, [P, PACK, CHUNK], F32) for q in range(4)]
@@ -169,7 +173,7 @@ def tile_picked_tshift_silu_po_kernel(
                 nc.tensor.matmul_mx(
                     out=acc[lo][t // per][:, t % per, :],
                     lhsT=w2w[:, P * t : P * t + P].bitcast(FP8X4),
-                    lhsT_scale=w2s[:, P * t : P * t + P],
+                    lhsT_scale=dealt["w2s"][:, P * t : P * t + P],
                     rhs=z_c[:].bitcast(FP8X4),
                     rhs_scale=z_s[:],
                     start=True,
@@ -188,6 +192,11 @@ def tile_picked_tshift_silu_po_kernel(
         def store(q):
             nc.sync.dma_start(out_rows[:, :, CHUNK * q : CHUNK * q + CHUNK], o_f[q][:])
 
+        def store_pair(q, pair):
+            nc.sync.dma_start(
+                out_rows[:, 2 * pair : 2 * pair + 2, CHUNK * q : CHUNK * q + CHUNK], o_f[q][:, 2 * pair : 2 * pair + 2, :]
+            )
+
         def weave(lo, hi):
             nc.vector.tensor_copy(
                 o_bf[:, PACK * lo : PACK * hi].rearrange("p (c i t) -> p c t i", i=4, t=PACK),
@@ -200,25 +209,40 @@ def tile_picked_tshift_silu_po_kernel(
         def words(lo, hi):
             nc.sync.dma_start(out_words[:, lo:hi], o_c[:, lo:hi].bitcast(I32))
 
+        first(0, 0, 0, "V")
+        first(1, 0, 1)
+        first(0, 1, 2)
+        first(1, 1, 3)
+        deal_words()
+        deal_bytes()
+        own_vec(0, 0)
+        own_vec(1, 0)
+        for t in (2, 3):
+            first(t, 0, 2 * t)
+            first(t, 1, 2 * t + 1)
+            own_part(t, 0)
+        for t in range(3):
+            wide(t)
         shift(0, (3,))
         act(0, 128)
-        second(0, 128, [6])
+        second(0, 128, [0, 1])
         shift(1, (3,))
-        leave(0, 128, "S")
-        store(0)
+        leave(0, 128, "SS")
+        store_pair(0, 0)
+        store_pair(0, 1)
         act(128, 256)
-        second(128, 256, [7])
+        second(128, 256, [4, 6])
         for t in range(PACK):
             own_part(t, 1)
-        leave(128, 256, "S")
+        leave(128, 256, "SS")
         store(1)
         shift(2, range(4))
         act(256, 384)
-        second(256, 384, [0])
+        second(256, 384, [2, 3])
         shift(3, range(4))
         act(384, 512)
-        second(384, 512, [1, 2])
-        leave(256, 384, "S")
+        second(384, 512, [5, 7])
+        leave(256, 384, "SS")
         store(2)
         leave(384, 512, "VS")
         store(3)

@@ -32,8 +32,8 @@ def tile_picked_tshift_silu_po_kernel(
         keep = ctx.enter_context(tc.tile_pool(name="keep", bufs=1))
         psum = ctx.enter_context(tc.psum_pool(name="psum", bufs=1))
 
-        def sb(name, shape, dtype, tag=None):
-            return keep.tile(shape, dtype, name=name, tag=tag or name, align_bytes=64)
+        def sb(name, shape, dtype):
+            return keep.tile(shape, dtype, name=name, tag=name, align_bytes=64)
 
         offs_t = sb("offs_t", [P, S // GROUP], U16)
         back_t = sb("back_t", [P, S // GROUP], U16)
@@ -62,10 +62,12 @@ def tile_picked_tshift_silu_po_kernel(
             nc.sync.dma_start(w2s_raw[r:P:32, :].bitcast(I32), w2s_rows[r].bitcast(I32))
         nc.sync.dma_start(back_t[:], back)
         nc.gpsimd.tensor_scalar(rest_t[:], mu_t[:], -1.0, 1.0, MULT, ADD)
+
         warm_in = sb("warm_in", [P, 1], F32)
         warm_out = sb("warm_out", [P, 1], F32)
         nc.vector.memset(warm_in[:], 0.0)
         nc.scalar.activation(warm_out[:], warm_in[:], SILU)
+
         xs = sb("xs", [P, S], U8)
         nc.vector.tensor_copy(xs[:], xs_all[:].indirect(offs_t[:]))
 
@@ -82,26 +84,13 @@ def tile_picked_tshift_silu_po_kernel(
         for h in range(2):
             nc.vector.tensor_copy(xw[:, HALF * h : HALF * h + HALF], xw_all[:].indirect(offs_t[:, 16 * h : 16 * h + 16]))
 
-
         y = {}
         win = [sb("win%d" % t, [P, S], F32) for t in range(PACK)]
         own = [sb("own%d" % t, [P, S], F32) for t in range(PACK)]
         halves = [slice(0, HALF), slice(HALF, S)]
         w2w = sb("w2w", [P, N], I32)
-        dealt = {}
 
-        def deal_words():
-            nc.gpsimd.tensor_copy(
-                w2w[:].rearrange("p (t c i) -> p c t i", t=PACK, i=4), w2w_raw[:].rearrange("p (c i t) -> p c t i", t=PACK, i=4)
-            )
-
-        def deal_bytes():
-            dealt["w2s"] = sb("w2s", [P, N], U8)
-            nc.gpsimd.tensor_copy(
-                dealt["w2s"][:].rearrange("p (t m) -> p t m", t=PACK), w2s_raw[:].rearrange("p (m t) -> p t m", t=PACK)
-            )
-
-        def first(t, h, bank, engine="S"):
+        def first(t, h, bank, on_vector=False):
             acc1 = psum.tile([P, HALF], F32, name="y%d" % bank, tag="bank%d" % bank)
             wcols = slice(P * (t % 2), P * (t % 2) + P)
             nc.tensor.matmul_mx(
@@ -113,17 +102,17 @@ def tile_picked_tshift_silu_po_kernel(
                 start=True,
                 stop=True,
             )
-            if engine == "V":
+            if on_vector:
                 nc.vector.tensor_scalar(win[t][:, halves[h]], acc1[:], rest_t[:, t : t + 1], None, MULT)
             else:
                 nc.scalar.activation(win[t][:, halves[h]], acc1[:], COPY, scale=rest_t[:, t : t + 1])
             y[t, h] = acc1[:]
 
-        def own_part(t, h):
-            nc.scalar.activation(own[t][:, halves[h]], y[t, h], COPY, scale=mu_t[:, t : t + 1])
-
-        def own_vec(t, h):
-            nc.vector.tensor_scalar(own[t][:, halves[h]], y[t, h], mu_t[:, t : t + 1], None, MULT)
+        def own_part(t, h, on_vector=False):
+            if on_vector:
+                nc.vector.tensor_scalar(own[t][:, halves[h]], y[t, h], mu_t[:, t : t + 1], None, MULT)
+            else:
+                nc.scalar.activation(own[t][:, halves[h]], y[t, h], COPY, scale=mu_t[:, t : t + 1])
 
         u_ring = sb("u_ring", [P, 11 * CHUNK], F32)
         u_half = u_ring[:, 3 * CHUNK : 11 * CHUNK].rearrange("p (t n) -> p t n", t=PACK)
@@ -134,21 +123,24 @@ def tile_picked_tshift_silu_po_kernel(
             u_half[:, :, CHUNK:HALF],
         ]
 
-        def wide(t):
+        def shift_half(t):
             nc.vector.tensor_tensor(u_half[:, t, :], win[t][:].indirect(back_t[:, 0:16]), own[t][:, halves[0]], ADD)
 
         def shift(q, ts):
             for t in ts:
                 nc.vector.tensor_tensor(
-                    u_q[q][:, t, :], win[t][:].indirect(back_t[:, 8 * q : 8 * q + 8]), own[t][:, CHUNK * q : CHUNK * q + CHUNK], ADD
+                    u_q[q][:, t, :],
+                    win[t][:].indirect(back_t[:, 8 * q : 8 * q + 8]),
+                    own[t][:, CHUNK * q : CHUNK * q + CHUNK],
+                    ADD,
                 )
-
 
         z_bf, acc = {}, {}
         o_f = [sb("o_f%d" % q, [P, PACK, CHUNK], F32) for q in range(4)]
         o_bf = sb("o_bf", [P, PACK * S], BF16)
         o_c = sb("o_c", [P, S], U32)
         o_s = sb("o_s", [P, S], U8)
+        w2s = sb("w2s", [P, N], U8)
         out_rows = out_0.rearrange("(p t) n -> p t n", t=PACK)
         out_words = out_1[0].rearrange("p n r -> p (n r)").bitcast(I32)
 
@@ -167,27 +159,21 @@ def tile_picked_tshift_silu_po_kernel(
             z_c = sb("z_c%d" % lo, [P, hi - lo], U32)
             z_s = sb("z_s%d" % lo, [P, hi - lo], U8)
             nc.vector.quantize_mx(out=z_c[:].bitcast(FP8X4), scales=z_s[:], in_=z_bf[lo][:])
-            per = PACK // len(banks)
-            acc[lo] = [psum.tile([P, per, hi - lo], F32, name="acc%d_%d" % (lo, b), tag="bank%d" % b) for b in banks]
+            acc[lo] = [psum.tile([P, 2, hi - lo], F32, name="acc%d_%d" % (lo, b), tag="bank%d" % b) for b in banks]
             for t in range(PACK):
                 nc.tensor.matmul_mx(
-                    out=acc[lo][t // per][:, t % per, :],
+                    out=acc[lo][t // 2][:, t % 2, :],
                     lhsT=w2w[:, P * t : P * t + P].bitcast(FP8X4),
-                    lhsT_scale=dealt["w2s"][:, P * t : P * t + P],
+                    lhsT_scale=w2s[:, P * t : P * t + P],
                     rhs=z_c[:].bitcast(FP8X4),
                     rhs_scale=z_s[:],
                     start=True,
                     stop=True,
                 )
 
-        def leave(lo, hi, engines):
-            per = PACK // len(engines)
-            for i in range(len(engines)):
-                dst = o_f[lo // CHUNK][:, per * i : per * i + per, within(lo, hi)]
-                if engines[i] == "V":
-                    nc.vector.tensor_copy(dst, acc[lo][i][:])
-                else:
-                    nc.scalar.copy(dst, acc[lo][i][:])
+        def leave(lo, copies):
+            for i in range(2):
+                copies[i](o_f[lo // CHUNK][:, 2 * i : 2 * i + 2, :], acc[lo][i][:])
 
         def store(q):
             nc.sync.dma_start(out_rows[:, :, CHUNK * q : CHUNK * q + CHUNK], o_f[q][:])
@@ -209,32 +195,40 @@ def tile_picked_tshift_silu_po_kernel(
         def words(lo, hi):
             nc.sync.dma_start(out_words[:, lo:hi], o_c[:, lo:hi].bitcast(I32))
 
-        first(0, 0, 0, "V")
+        by_scalar = (nc.scalar.copy, nc.scalar.copy)
+
+        first(0, 0, 0, on_vector=True)
         first(1, 0, 1)
         first(0, 1, 2)
         first(1, 1, 3)
-        deal_words()
-        deal_bytes()
-        own_vec(0, 0)
-        own_vec(1, 0)
+        nc.gpsimd.tensor_copy(
+            w2w[:].rearrange("p (t c i) -> p c t i", t=PACK, i=4),
+            w2w_raw[:].rearrange("p (c i t) -> p c t i", t=PACK, i=4),
+        )
+        nc.gpsimd.tensor_copy(
+            w2s[:].rearrange("p (t m) -> p t m", t=PACK), w2s_raw[:].rearrange("p (m t) -> p t m", t=PACK)
+        )
+        own_part(0, 0, on_vector=True)
+        own_part(1, 0, on_vector=True)
         for t in (2, 3):
             first(t, 0, 2 * t)
             first(t, 1, 2 * t + 1)
             own_part(t, 0)
         for t in range(3):
-            wide(t)
+            shift_half(t)
+
         shift(0, (3,))
         act(0, 128)
         second(0, 128, [0, 1])
         shift(1, (3,))
-        leave(0, 128, "SS")
+        leave(0, by_scalar)
         store_pair(0, 0)
         store_pair(0, 1)
         act(128, 256)
         second(128, 256, [4, 6])
         for t in range(PACK):
             own_part(t, 1)
-        leave(128, 256, "SS")
+        leave(128, by_scalar)
         store(1)
         shift(2, range(4))
         act(256, 384)
@@ -242,10 +236,11 @@ def tile_picked_tshift_silu_po_kernel(
         shift(3, range(4))
         act(384, 512)
         second(384, 512, [5, 7])
-        leave(256, 384, "SS")
+        leave(256, by_scalar)
         store(2)
-        leave(384, 512, "VS")
+        leave(384, (nc.vector.tensor_copy, nc.scalar.copy))
         store(3)
+
         weave(0, 128)
         weave(128, 256)
         planes(0, 128)

@@ -22,6 +22,7 @@ PACK = 4
 HALF = S // 2
 CHUNK = S // 4
 GROUP = 16
+REGION = 64 * 1024
 
 
 def tile_picked_tshift_silu_po_kernel(
@@ -29,14 +30,22 @@ def tile_picked_tshift_silu_po_kernel(
 ):
     nc = tc.nc
     with ExitStack() as ctx:
+        lists = ctx.enter_context(tc.tile_pool(name="lists", bufs=1))
         keep = ctx.enter_context(tc.tile_pool(name="keep", bufs=1))
         psum = ctx.enter_context(tc.psum_pool(name="psum", bufs=1))
 
-        def sb(name, shape, dtype):
-            return keep.tile(shape, dtype, name=name, tag=name, align_bytes=64)
+        free = [REGION * i for i in range(4)]
 
-        offs_t = sb("offs_t", [P, S // GROUP], U16)
-        back_t = sb("back_t", [P, S // GROUP], U16)
+        def sb(name, shape, dtype, region=0):
+            at = free[region]
+            size = 1 if dtype == U8 else 2 if dtype == BF16 else 4
+            for extent in shape[1:]:
+                size = size * extent
+            free[region] = at + (size + 63) // 64 * 64
+            return keep.tile(shape, dtype, name=name, tag=name, align_bytes=64, offset=at)
+
+        offs_t = lists.tile([P, S // GROUP], U16, name="offs_t", tag="offs_t")
+        back_t = lists.tile([P, S // GROUP], U16, name="back_t", tag="back_t")
         w1_raw = sb("w1_raw", [P, PACK, H], F32)
         xw_all = sb("xw_all", [P, T], U32)
         xs_all = sb("xs_all", [P, T], U8)
@@ -68,10 +77,10 @@ def tile_picked_tshift_silu_po_kernel(
         nc.vector.memset(warm_in[:], 0.0)
         nc.scalar.activation(warm_out[:], warm_in[:], SILU)
 
-        xs = sb("xs", [P, S], U8)
+        xs = sb("xs", [P, S], U8, 2)
         nc.vector.tensor_copy(xs[:], xs_all[:].indirect(offs_t[:]))
 
-        w1_bf = [sb("w1_bf%d" % u, [P, 2 * P * PACK], BF16) for u in range(2)]
+        w1_bf = [sb("w1_bf%d" % u, [P, 2 * P * PACK], BF16, 3) for u in range(2)]
         w1_c = [sb("w1_c%d" % u, [P, 2 * P], U32) for u in range(2)]
         w1_s = [sb("w1_s%d" % u, [P, 2 * P], U8) for u in range(2)]
         src = w1_raw[:].rearrange("p j (m t) -> p m j t", t=PACK)
@@ -80,13 +89,13 @@ def tile_picked_tshift_silu_po_kernel(
         for u in range(2):
             nc.vector.quantize_mx(out=w1_c[u][:].bitcast(FP8X4), scales=w1_s[u][:], in_=w1_bf[u][:])
 
-        xw = sb("xw", [P, S], U32)
+        xw = sb("xw", [P, S], U32, 1)
         for h in range(2):
             nc.vector.tensor_copy(xw[:, HALF * h : HALF * h + HALF], xw_all[:].indirect(offs_t[:, 16 * h : 16 * h + 16]))
 
         y = {}
-        win = [sb("win%d" % t, [P, S], F32) for t in range(PACK)]
-        own = [sb("own%d" % t, [P, S], F32) for t in range(PACK)]
+        win = [sb("win%d" % t, [P, S], F32, 1) for t in range(PACK)]
+        own = [sb("own%d" % t, [P, S], F32, 2) for t in range(PACK)]
         halves = [slice(0, HALF), slice(HALF, S)]
         w2w = sb("w2w", [P, N], I32)
 
@@ -114,7 +123,7 @@ def tile_picked_tshift_silu_po_kernel(
             else:
                 nc.scalar.activation(own[t][:, halves[h]], y[t, h], COPY, scale=mu_t[:, t : t + 1])
 
-        u_ring = sb("u_ring", [P, 11 * CHUNK], F32)
+        u_ring = sb("u_ring", [P, 11 * CHUNK], F32, 3)
         u_half = u_ring[:, 3 * CHUNK : 11 * CHUNK].rearrange("p (t n) -> p t n", t=PACK)
         u_q = [
             u_half[:, :, 0:CHUNK],
@@ -137,9 +146,9 @@ def tile_picked_tshift_silu_po_kernel(
 
         z_bf, acc = {}, {}
         o_f = [sb("o_f%d" % q, [P, PACK, CHUNK], F32) for q in range(4)]
-        o_bf = sb("o_bf", [P, PACK * S], BF16)
-        o_c = sb("o_c", [P, S], U32)
-        o_s = sb("o_s", [P, S], U8)
+        o_bf = sb("o_bf", [P, PACK * S], BF16, 1)
+        o_c = sb("o_c", [P, S], U32, 2)
+        o_s = sb("o_s", [P, S], U8, 3)
         w2s = sb("w2s", [P, N], U8)
         out_rows = out_0.rearrange("(p t) n -> p t n", t=PACK)
         out_words = out_1[0].rearrange("p n r -> p (n r)").bitcast(I32)
@@ -148,7 +157,7 @@ def tile_picked_tshift_silu_po_kernel(
             return slice(lo % CHUNK, lo % CHUNK + hi - lo)
 
         def act(lo, hi):
-            z_bf[lo] = sb("z_bf%d" % lo, [P, PACK * (hi - lo)], BF16)
+            z_bf[lo] = sb("z_bf%d" % lo, [P, PACK * (hi - lo)], BF16, 2)
             nc.scalar.activation(
                 z_bf[lo][:].rearrange("p (c i t) -> p c t i", i=4, t=PACK),
                 u_q[lo // CHUNK][:, :, within(lo, hi)].rearrange("p t (c i) -> p c t i", i=4),

@@ -41,8 +41,8 @@ def tile_picked_tshift_silu_po_kernel(
             size = 1 if dtype == U8 else 2 if dtype == BF16 else 4
             for extent in shape[1:]:
                 size = size * extent
-            free[region] = at + (size + 63) // 64 * 64
-            return keep.tile(shape, dtype, name=name, tag=name, align_bytes=64, offset=at)
+            free[region] = at + (size + 255) // 256 * 256
+            return keep.tile(shape, dtype, name=name, tag=name, align_bytes=256, offset=at)
 
         offs_t = lists.tile([P, S // GROUP], U16, name="offs_t", tag="offs_t")
         back_t = lists.tile([P, S // GROUP], U16, name="back_t", tag="back_t")
@@ -90,38 +90,37 @@ def tile_picked_tshift_silu_po_kernel(
             nc.vector.quantize_mx(out=w1_c[u][:].bitcast(FP8X4), scales=w1_s[u][:], in_=w1_bf[u][:])
 
         xw = sb("xw", [P, S], U32, 1)
+        chunks = [slice(CHUNK * q, CHUNK * q + CHUNK) for q in range(4)]
+        halves = [slice(0, HALF), slice(HALF, S)]
         for h in range(2):
-            nc.vector.tensor_copy(xw[:, HALF * h : HALF * h + HALF], xw_all[:].indirect(offs_t[:, 16 * h : 16 * h + 16]))
+            nc.vector.tensor_copy(xw[:, halves[h]], xw_all[:].indirect(offs_t[:, 16 * h : 16 * h + 16]))
 
-        y = {}
         win = [sb("win%d" % t, [P, S], F32, 1) for t in range(PACK)]
         own = [sb("own%d" % t, [P, S], F32, 2) for t in range(PACK)]
-        halves = [slice(0, HALF), slice(HALF, S)]
         w2w = sb("w2w", [P, N], I32)
+        w2s = sb("w2s", [P, N], U8)
+        y = {}
+        for t in range(PACK):
+            for h in range(2):
+                y[t, h] = psum.tile([P, HALF], F32, name="y%d_%d" % (t, h), tag="bank%d" % (2 * t + h))
 
-        def first(t, h, bank, on_vector=False):
-            acc1 = psum.tile([P, HALF], F32, name="y%d" % bank, tag="bank%d" % bank)
+        def first(t, lo, hi):
             wcols = slice(P * (t % 2), P * (t % 2) + P)
             nc.tensor.matmul_mx(
-                out=acc1[:],
+                out=y[t, lo // HALF][:, lo % HALF : lo % HALF + hi - lo],
                 lhsT=w1_c[t // 2][:, wcols].bitcast(FP8X4),
                 lhsT_scale=w1_s[t // 2][:, wcols],
-                rhs=xw[:, halves[h]].bitcast(FP8X4),
-                rhs_scale=xs[:, halves[h]],
+                rhs=xw[:, lo:hi].bitcast(FP8X4),
+                rhs_scale=xs[:, lo:hi],
                 start=True,
                 stop=True,
             )
-            if on_vector:
-                nc.vector.tensor_scalar(win[t][:, halves[h]], acc1[:], rest_t[:, t : t + 1], None, MULT)
-            else:
-                nc.scalar.activation(win[t][:, halves[h]], acc1[:], COPY, scale=rest_t[:, t : t + 1])
-            y[t, h] = acc1[:]
 
-        def own_part(t, h, on_vector=False):
-            if on_vector:
-                nc.vector.tensor_scalar(own[t][:, halves[h]], y[t, h], mu_t[:, t : t + 1], None, MULT)
+        def scaled(out, t, h, factor):
+            if t == 0:
+                nc.vector.tensor_scalar(out[t][:, halves[h]], y[t, h][:], factor[:, t : t + 1], None, MULT)
             else:
-                nc.scalar.activation(own[t][:, halves[h]], y[t, h], COPY, scale=mu_t[:, t : t + 1])
+                nc.scalar.activation(out[t][:, halves[h]], y[t, h][:], COPY, scale=factor[:, t : t + 1])
 
         u_ring = sb("u_ring", [P, 11 * CHUNK], F32, 3)
         u_half = u_ring[:, 3 * CHUNK : 11 * CHUNK].rearrange("p (t n) -> p t n", t=PACK)
@@ -135,67 +134,53 @@ def tile_picked_tshift_silu_po_kernel(
         def shift_half(t):
             nc.vector.tensor_tensor(u_half[:, t, :], win[t][:].indirect(back_t[:, 0:16]), own[t][:, halves[0]], ADD)
 
-        def shift(q, ts):
-            for t in ts:
-                nc.vector.tensor_tensor(
-                    u_q[q][:, t, :],
-                    win[t][:].indirect(back_t[:, 8 * q : 8 * q + 8]),
-                    own[t][:, CHUNK * q : CHUNK * q + CHUNK],
-                    ADD,
-                )
+        def shift(q, t):
+            nc.vector.tensor_tensor(
+                u_q[q][:, t, :], win[t][:].indirect(back_t[:, 8 * q : 8 * q + 8]), own[t][:, chunks[q]], ADD
+            )
 
-        z_bf, acc = {}, {}
+        z_bf = [sb("z_bf%d" % q, [P, PACK * CHUNK], BF16, 2) for q in range(4)]
+        z_c = [sb("z_c%d" % q, [P, CHUNK], U32) for q in range(4)]
+        z_s = [sb("z_s%d" % q, [P, CHUNK], U8) for q in range(4)]
         o_f = [sb("o_f%d" % q, [P, PACK, CHUNK], F32) for q in range(4)]
         o_bf = sb("o_bf", [P, PACK * S], BF16, 1)
         o_c = sb("o_c", [P, S], U32, 2)
         o_s = sb("o_s", [P, S], U8, 3)
-        w2s = sb("w2s", [P, N], U8)
         out_rows = out_0.rearrange("(p t) n -> p t n", t=PACK)
         out_words = out_1[0].rearrange("p n r -> p (n r)").bitcast(I32)
+        acc = {}
 
-        def within(lo, hi):
-            return slice(lo % CHUNK, lo % CHUNK + hi - lo)
-
-        def act(lo, hi):
-            z_bf[lo] = sb("z_bf%d" % lo, [P, PACK * (hi - lo)], BF16, 2)
+        def act(q):
             nc.scalar.activation(
-                z_bf[lo][:].rearrange("p (c i t) -> p c t i", i=4, t=PACK),
-                u_q[lo // CHUNK][:, :, within(lo, hi)].rearrange("p t (c i) -> p c t i", i=4),
+                z_bf[q][:].rearrange("p (c i t) -> p c t i", i=4, t=PACK),
+                u_q[q].rearrange("p t (c i) -> p c t i", i=4),
                 SILU,
             )
 
-        def second(lo, hi, banks):
-            z_c = sb("z_c%d" % lo, [P, hi - lo], U32)
-            z_s = sb("z_s%d" % lo, [P, hi - lo], U8)
-            nc.vector.quantize_mx(out=z_c[:].bitcast(FP8X4), scales=z_s[:], in_=z_bf[lo][:])
-            acc[lo] = [psum.tile([P, 2, hi - lo], F32, name="acc%d_%d" % (lo, b), tag="bank%d" % b) for b in banks]
+        def second(q, banks):
+            nc.vector.quantize_mx(out=z_c[q][:].bitcast(FP8X4), scales=z_s[q][:], in_=z_bf[q][:])
+            acc[q] = [psum.tile([P, 2, CHUNK], F32, name="acc%d_%d" % (q, b), tag="bank%d" % b) for b in banks]
             for t in range(PACK):
                 nc.tensor.matmul_mx(
-                    out=acc[lo][t // 2][:, t % 2, :],
+                    out=acc[q][t // 2][:, t % 2, :],
                     lhsT=w2w[:, P * t : P * t + P].bitcast(FP8X4),
                     lhsT_scale=w2s[:, P * t : P * t + P],
-                    rhs=z_c[:].bitcast(FP8X4),
-                    rhs_scale=z_s[:],
+                    rhs=z_c[q][:].bitcast(FP8X4),
+                    rhs_scale=z_s[q][:],
                     start=True,
                     stop=True,
                 )
 
-        def leave(lo, copies):
-            for i in range(2):
-                copies[i](o_f[lo // CHUNK][:, 2 * i : 2 * i + 2, :], acc[lo][i][:])
+        def leave(q, pair, copy):
+            copy(o_f[q][:, 2 * pair : 2 * pair + 2, :], acc[q][pair][:])
 
-        def store(q):
-            nc.sync.dma_start(out_rows[:, :, CHUNK * q : CHUNK * q + CHUNK], o_f[q][:])
-
-        def store_pair(q, pair):
-            nc.sync.dma_start(
-                out_rows[:, 2 * pair : 2 * pair + 2, CHUNK * q : CHUNK * q + CHUNK], o_f[q][:, 2 * pair : 2 * pair + 2, :]
-            )
+        def store(q, lo=0, hi=PACK):
+            nc.sync.dma_start(out_rows[:, lo:hi, chunks[q]], o_f[q][:, lo:hi, :])
 
         def weave(lo, hi):
             nc.vector.tensor_copy(
                 o_bf[:, PACK * lo : PACK * hi].rearrange("p (c i t) -> p c t i", i=4, t=PACK),
-                o_f[lo // CHUNK][:, :, within(lo, hi)].rearrange("p t (c i) -> p c t i", i=4),
+                o_f[lo // CHUNK][:, :, lo % CHUNK : lo % CHUNK + hi - lo].rearrange("p t (c i) -> p c t i", i=4),
             )
 
         def planes(lo, hi):
@@ -204,12 +189,12 @@ def tile_picked_tshift_silu_po_kernel(
         def words(lo, hi):
             nc.sync.dma_start(out_words[:, lo:hi], o_c[:, lo:hi].bitcast(I32))
 
-        by_scalar = (nc.scalar.copy, nc.scalar.copy)
-
-        first(0, 0, 0, on_vector=True)
-        first(1, 0, 1)
-        first(0, 1, 2)
-        first(1, 1, 3)
+        for h in range(2):
+            for t in range(2):
+                first(t, HALF * h, HALF * h + HALF)
+        for t in (2, 3):
+            for h in range(2):
+                first(t, HALF * h, HALF * h + HALF)
         nc.gpsimd.tensor_copy(
             w2w[:].rearrange("p (t c i) -> p c t i", t=PACK, i=4),
             w2w_raw[:].rearrange("p (c i t) -> p c t i", t=PACK, i=4),
@@ -217,37 +202,48 @@ def tile_picked_tshift_silu_po_kernel(
         nc.gpsimd.tensor_copy(
             w2s[:].rearrange("p (t m) -> p t m", t=PACK), w2s_raw[:].rearrange("p (m t) -> p t m", t=PACK)
         )
-        own_part(0, 0, on_vector=True)
-        own_part(1, 0, on_vector=True)
+
+        for h in range(2):
+            scaled(win, 0, h, rest_t)
+            scaled(own, 0, h, mu_t)
+        scaled(win, 1, 0, rest_t)
+        scaled(own, 1, 0, mu_t)
+        scaled(win, 1, 1, rest_t)
         for t in (2, 3):
-            first(t, 0, 2 * t)
-            first(t, 1, 2 * t + 1)
-            own_part(t, 0)
+            scaled(win, t, 0, rest_t)
+            scaled(win, t, 1, rest_t)
+            scaled(own, t, 0, mu_t)
+        for t in (1, 2, 3):
+            scaled(own, t, 1, mu_t)
+
         for t in range(3):
             shift_half(t)
-
-        shift(0, (3,))
-        act(0, 128)
-        second(0, 128, [0, 1])
-        shift(1, (3,))
-        leave(0, by_scalar)
-        store_pair(0, 0)
-        store_pair(0, 1)
-        act(128, 256)
-        second(128, 256, [4, 6])
+        shift(0, 3)
+        shift(1, 3)
+        for t in range(3):
+            shift(2, t)
+        act(0)
+        second(0, [0, 2])
+        shift(2, 3)
+        act(1)
+        second(1, [1, 4])
+        act(2)
         for t in range(PACK):
-            own_part(t, 1)
-        leave(128, by_scalar)
+            shift(3, t)
+        second(2, [6, 3])
+        for pair in range(2):
+            leave(0, pair, nc.scalar.copy)
+            store(0, 2 * pair, 2 * pair + 2)
+        leave(1, 0, nc.scalar.copy)
+        leave(1, 1, nc.scalar.copy)
         store(1)
-        shift(2, range(4))
-        act(256, 384)
-        second(256, 384, [2, 3])
-        shift(3, range(4))
-        act(384, 512)
-        second(384, 512, [5, 7])
-        leave(256, by_scalar)
+        act(3)
+        second(3, [5, 7])
+        for pair in range(2):
+            leave(2, pair, nc.scalar.copy)
         store(2)
-        leave(384, (nc.vector.tensor_copy, nc.scalar.copy))
+        leave(3, 0, nc.vector.tensor_copy)
+        leave(3, 1, nc.scalar.copy)
         store(3)
 
         weave(0, 128)

from contextlib import ExitStack

import concourse.mybir as mybir

K, T, S, N, H = 512, 2048, 512, 512, 512
FLOPS = 2 * K * H * S + 2 * H * N * S

F32 = mybir.dt.float32
BF16 = mybir.dt.bfloat16
I32 = mybir.dt.int32
U32 = mybir.dt.uint32
U16 = mybir.dt.uint16
U8 = mybir.dt.uint8
FP8X4 = mybir.dt.float8_e4m3fn_x4
MULT = mybir.AluOpType.mult
ADD = mybir.AluOpType.add
COPY = mybir.ActivationFunctionType.Copy
SILU = mybir.ActivationFunctionType.Silu

P = 128
PACK = 4
HALF = S // 2
CHUNK = S // 4
GROUP = 16
REGION = 64 * 1024


def tile_picked_tshift_silu_po_kernel(
    tc, x_words, x_scales, w1, mu, w2_words, w2_scales, offs, back, out_0, out_1, out_2
):
    nc = tc.nc
    with ExitStack() as ctx:
        lists = ctx.enter_context(tc.tile_pool(name="lists", bufs=1))
        keep = ctx.enter_context(tc.tile_pool(name="keep", bufs=1))
        psum = ctx.enter_context(tc.psum_pool(name="psum", bufs=1))

        free = [REGION * i for i in range(4)]

        def sb(name, shape, dtype, region=0):
            at = free[region]
            size = 1 if dtype == U8 else 2 if dtype == BF16 else 4
            for extent in shape[1:]:
                size = size * extent
            free[region] = at + (size + 255) // 256 * 256
            return keep.tile(shape, dtype, name=name, tag=name, align_bytes=256, offset=at)

        offs_t = lists.tile([P, S // GROUP], U16, name="offs_t", tag="offs_t")
        back_t = lists.tile([P, S // GROUP], U16, name="back_t", tag="back_t")
        w1_raw = sb("w1_raw", [P, PACK, H], F32)
        xw_all = sb("xw_all", [P, T], U32)
        xs_all = sb("xs_all", [P, T], U8)
        w2w_raw = sb("w2w_raw", [P, N], I32)
        w2s_raw = sb("w2s_raw", [P, N], U8)
        mu_t = sb("mu_t", [P, PACK], F32)
        rest_t = sb("rest_t", [P, PACK], F32)

        nc.gpsimd.memset(xs_all[:].bitcast(I32), 0)
        nc.vector.memset(w2s_raw[:].bitcast(I32), 0)
        w1_rows = w1.rearrange("(p j) c -> p j c", j=PACK)
        nc.sync.dma_start(w1_raw[:, 0:2, :], w1_rows[:, 0:2, :])
        nc.sync.dma_start(offs_t[:], offs)
        xs_rows = x_scales[0].rearrange("(q r) n -> r q n", r=4)
        for r in range(4):
            nc.sync.dma_start(xs_all[r:P:32, :].bitcast(I32), xs_rows[r].bitcast(I32))
        nc.sync.dma_start(w1_raw[:, 2:4, :], w1_rows[:, 2:4, :])
        nc.sync.dma_start(xw_all[:].bitcast(I32), x_words[0].rearrange("p n r -> p (n r)").bitcast(I32))
        nc.sync.dma_start(mu_t[:], mu.rearrange("(p t) o -> p (t o)", t=PACK))
        nc.sync.dma_start(w2w_raw[:], w2_words[0].rearrange("p n r -> p (n r)").bitcast(I32))
        w2s_rows = w2_scales[0].rearrange("(q r) n -> r q n", r=4)
        for r in range(4):
            nc.sync.dma_start(w2s_raw[r:P:32, :].bitcast(I32), w2s_rows[r].bitcast(I32))
        nc.sync.dma_start(back_t[:], back)
        nc.gpsimd.tensor_scalar(rest_t[:], mu_t[:], -1.0, 1.0, MULT, ADD)

        warm_in = sb("warm_in", [P, 1], F32)
        warm_out = sb("warm_out", [P, 1], F32)
        nc.vector.memset(warm_in[:], 0.0)
        nc.scalar.activation(warm_out[:], warm_in[:], SILU)

        xs = sb("xs", [P, S], U8, 2)
        nc.vector.tensor_copy(xs[:], xs_all[:].indirect(offs_t[:]))

        w1_bf = [sb("w1_bf%d" % u, [P, 2 * P * PACK], BF16, 3) for u in range(2)]
        w1_c = [sb("w1_c%d" % u, [P, 2 * P], U32) for u in range(2)]
        w1_s = [sb("w1_s%d" % u, [P, 2 * P], U8) for u in range(2)]
        src = w1_raw[:].rearrange("p j (m t) -> p m j t", t=PACK)
        nc.vector.tensor_copy(w1_bf[0][:].rearrange("p (t m j) -> p m j t", t=2, j=PACK), src[:, :, :, 0:2])
        nc.scalar.copy(w1_bf[1][:].rearrange("p (t m j) -> p m j t", t=2, j=PACK), src[:, :, :, 2:4])
        for u in range(2):
            nc.vector.quantize_mx(out=w1_c[u][:].bitcast(FP8X4), scales=w1_s[u][:], in_=w1_bf[u][:])

        xw = sb("xw", [P, S], U32, 1)
        chunks = [slice(CHUNK * q, CHUNK * q + CHUNK) for q in range(4)]
        halves = [slice(0, HALF), slice(HALF, S)]
        for h in range(2):
            nc.vector.tensor_copy(xw[:, halves[h]], xw_all[:].indirect(offs_t[:, 16 * h : 16 * h + 16]))

        win = [sb("win%d" % t, [P, S], F32, 1) for t in range(PACK)]
        own = [sb("own%d" % t, [P, S], F32, 2) for t in range(PACK)]
        w2w = sb("w2w", [P, N], I32)
        w2s = sb("w2s", [P, N], U8)
        y = {}
        for t in range(PACK):
            for h in range(2):
                y[t, h] = psum.tile([P, HALF], F32, name="y%d_%d" % (t, h), tag="bank%d" % (2 * t + h))

        def first(t, lo, hi):
            wcols = slice(P * (t % 2), P * (t % 2) + P)
            nc.tensor.matmul_mx(
                out=y[t, lo // HALF][:, lo % HALF : lo % HALF + hi - lo],
                lhsT=w1_c[t // 2][:, wcols].bitcast(FP8X4),
                lhsT_scale=w1_s[t // 2][:, wcols],
                rhs=xw[:, lo:hi].bitcast(FP8X4),
                rhs_scale=xs[:, lo:hi],
                start=True,
                stop=True,
            )

        def scaled(out, t, h, factor):
            if t == 0:
                nc.vector.tensor_scalar(out[t][:, halves[h]], y[t, h][:], factor[:, t : t + 1], None, MULT)
            else:
                nc.scalar.activation(out[t][:, halves[h]], y[t, h][:], COPY, scale=factor[:, t : t + 1])

        u_ring = sb("u_ring", [P, 11 * CHUNK], F32, 3)
        u_half = u_ring[:, 3 * CHUNK : 11 * CHUNK].rearrange("p (t n) -> p t n", t=PACK)
        u_q = [
            u_half[:, :, 0:CHUNK],
            u_half[:, :, CHUNK:HALF],
            u_ring[:, 0 : PACK * CHUNK].rearrange("p (t n) -> p t n", t=PACK),
            u_half[:, :, CHUNK:HALF],
        ]

        def shift_half(t):
            nc.vector.tensor_tensor(u_half[:, t, :], win[t][:].indirect(back_t[:, 0:16]), own[t][:, halves[0]], ADD)

        def shift(q, t):
            nc.vector.tensor_tensor(
                u_q[q][:, t, :], win[t][:].indirect(back_t[:, 8 * q : 8 * q + 8]), own[t][:, chunks[q]], ADD
            )

        z_bf = [sb("z_bf%d" % q, [P, PACK * CHUNK], BF16, 2) for q in range(4)]
        z_c = [sb("z_c%d" % q, [P, CHUNK], U32) for q in range(4)]
        z_s = [sb("z_s%d" % q, [P, CHUNK], U8) for q in range(4)]
        o_f = [sb("o_f%d" % q, [P, PACK, CHUNK], F32) for q in range(4)]
        o_bf = sb("o_bf", [P, PACK * S], BF16, 1)
        o_c = sb("o_c", [P, S], U32, 2)
        o_s = sb("o_s", [P, S], U8, 3)
        out_rows = out_0.rearrange("(p t) n -> p t n", t=PACK)
        out_words = out_1[0].rearrange("p n r -> p (n r)").bitcast(I32)
        acc = {}

        def act(q):
            nc.scalar.activation(
                z_bf[q][:].rearrange("p (c i t) -> p c t i", i=4, t=PACK),
                u_q[q].rearrange("p t (c i) -> p c t i", i=4),
                SILU,
            )

        def second(q, banks):
            nc.vector.quantize_mx(out=z_c[q][:].bitcast(FP8X4), scales=z_s[q][:], in_=z_bf[q][:])
            acc[q] = [psum.tile([P, 2, CHUNK], F32, name="acc%d_%d" % (q, b), tag="bank%d" % b) for b in banks]
            for t in range(PACK):
                nc.tensor.matmul_mx(
                    out=acc[q][t // 2][:, t % 2, :],
                    lhsT=w2w[:, P * t : P * t + P].bitcast(FP8X4),
                    lhsT_scale=w2s[:, P * t : P * t + P],
                    rhs=z_c[q][:].bitcast(FP8X4),
                    rhs_scale=z_s[q][:],
                    start=True,
                    stop=True,
                )

        def leave(q, pair, copy):
            copy(o_f[q][:, 2 * pair : 2 * pair + 2, :], acc[q][pair][:])

        def store(q, lo=0, hi=PACK):
            nc.sync.dma_start(out_rows[:, lo:hi, chunks[q]], o_f[q][:, lo:hi, :])

        def weave(lo, hi):
            nc.vector.tensor_copy(
                o_bf[:, PACK * lo : PACK * hi].rearrange("p (c i t) -> p c t i", i=4, t=PACK),
                o_f[lo // CHUNK][:, :, lo % CHUNK : lo % CHUNK + hi - lo].rearrange("p t (c i) -> p c t i", i=4),
            )

        def planes(lo, hi):
            nc.vector.quantize_mx(out=o_c[:, lo:hi].bitcast(FP8X4), scales=o_s[:, lo:hi], in_=o_bf[:, PACK * lo : PACK * hi])

        def words(lo, hi):
            nc.sync.dma_start(out_words[:, lo:hi], o_c[:, lo:hi].bitcast(I32))

        for h in range(2):
            for t in range(2):
                first(t, HALF * h, HALF * h + HALF)
        for t in (2, 3):
            for h in range(2):
                first(t, HALF * h, HALF * h + HALF)
        nc.gpsimd.tensor_copy(
            w2w[:].rearrange("p (t c i) -> p c t i", t=PACK, i=4),
            w2w_raw[:].rearrange("p (c i t) -> p c t i", t=PACK, i=4),
        )
        nc.gpsimd.tensor_copy(
            w2s[:].rearrange("p (t m) -> p t m", t=PACK), w2s_raw[:].rearrange("p (m t) -> p t m", t=PACK)
        )

        for h in range(2):
            scaled(win, 0, h, rest_t)
            scaled(own, 0, h, mu_t)
        scaled(win, 1, 0, rest_t)
        scaled(own, 1, 0, mu_t)
        scaled(win, 1, 1, rest_t)
        for t in (2, 3):
            scaled(win, t, 0, rest_t)
            scaled(win, t, 1, rest_t)
            scaled(own, t, 0, mu_t)
        for t in (1, 2, 3):
            scaled(own, t, 1, mu_t)

        for t in range(3):
            shift_half(t)
        shift(0, 3)
        shift(1, 3)
        for t in range(3):
            shift(2, t)
        act(0)
        second(0, [0, 2])
        shift(2, 3)
        act(1)
        second(1, [1, 4])
        act(2)
        for t in range(PACK):
            shift(3, t)
        second(2, [6, 3])
        for pair in range(2):
            leave(0, pair, nc.scalar.copy)
            store(0, 2 * pair, 2 * pair + 2)
        leave(1, 0, nc.scalar.copy)
        leave(1, 1, nc.scalar.copy)
        store(1)
        act(3)
        second(3, [5, 7])
        for pair in range(2):
            leave(2, pair, nc.scalar.copy)
        store(2)
        leave(3, 0, nc.vector.tensor_copy)
        leave(3, 1, nc.scalar.copy)
        store(3)

        weave(0, 128)
        weave(128, 256)
        planes(0, 128)
        planes(128, 256)
        words(0, 256)
        weave(256, 384)
        weave(384, 448)
        planes(256, 384)
        weave(448, 512)
        planes(384, 448)
        planes(448, 512)
        words(256, 512)
        out_scales = out_2[0].rearrange("(q r) n -> r q n", r=4)
        for r in range(4):
            eng = nc.scalar if r % 2 == 0 else nc.sync
            eng.dma_start(out_scales[r].bitcast(I32), o_s[r:P:32, :].bitcast(I32))
